import numpy as np
import ml_dtypes


def mxq(x, axis, fmt="e4m3"):
    dtype, down = {"e4m3": (ml_dtypes.float8_e4m3fn, 7), "e5m2": (ml_dtypes.float8_e5m2, 14)}[fmt]
    v = np.moveaxis(np.asarray(x, np.float32).astype(ml_dtypes.bfloat16).astype(np.float64), axis, -1)
    blocks = v.reshape(v.shape[:-1] + (-1, 32))
    amax = np.abs(blocks).max(-1, keepdims=True)
    byte = np.maximum(np.where(amax > 0, np.frexp(amax)[1] - 1 + 127, 0) - down, 1)
    scale = np.exp2(byte - 127.0)
    codes = (blocks / scale).astype(np.float32).astype(dtype).astype(np.float64)
    return np.moveaxis((codes * scale).reshape(v.shape), -1, axis)


WIDE = False


def mx_kscale(k):
    if not WIDE:
        return np.ones(k)
    levels = np.array([30, -30])
    if k % 512:
        return np.exp2(np.random.permutation(np.resize(levels, k // 32))).repeat(32)
    a = np.empty((k // 512, 16))
    for p in range(k // 512):
        a[p, :8] = np.random.permutation(np.resize(levels, 8))
        for g in range(8):
            far = levels[np.abs(levels - a[p, g]) >= 10]
            a[p, g + 8] = far[np.random.randint(len(far))]
    return np.exp2(a.ravel()).repeat(32)


def f64(x):
    return np.asarray(x).astype(np.float64)


def striped(idx):
    return np.tile(np.asarray(idx).reshape(-1, 16).T, (8, 1)).astype(np.uint16)


def unstriped(offs):
    return offs[:16].T.reshape(-1).astype(np.int64)


def striped8(idx):
    return np.asarray(idx).reshape(8, -1, 16).transpose(0, 2, 1).reshape(128, -1).astype(np.uint16)


def unstriped8(offs):
    return offs.reshape(8, 16, -1).transpose(0, 2, 1).reshape(8, -1).astype(np.int64)


def pick8(x, idx, run):
    r = np.arange(len(x))
    return x[r[:, None], idx[r % (8 * run) // run]]


E2M1 = np.array([0.0, 0.5, 1.0, 1.5, 2.0, 3.0, 4.0, 6.0, -0.0, -0.5, -1.0, -1.5, -2.0, -3.0, -4.0, -6.0])


def pack_weight(w, fmt):
    k, n = w.shape
    w = f64(np.asarray(w, np.float32).astype(ml_dtypes.bfloat16)).reshape(k // 32, 32, n)
    amax = np.abs(w).max(1)
    if fmt in ("e4m3", "e5m2"):
        byte = np.frexp(amax)[1] - 1 + 127 - (7 if fmt == "e4m3" else 14)
    else:
        mant, ex = np.frexp(amax / 6.0)
        byte = np.where(mant > 0.5, ex, ex - 1) + 127
    byte = np.clip(np.where(amax > 0, byte, 1), 1, 254)
    scaled = (w * np.exp2(127.0 - byte)[:, None, :]).reshape(k, n).astype(np.float32)
    by_word = np.ascontiguousarray(scaled.reshape(k // 512, 128, 4, n).transpose(0, 1, 3, 2))
    if fmt in ("e4m3", "e5m2"):
        words = by_word.astype(ml_dtypes.float8_e4m3fn if fmt == "e4m3" else ml_dtypes.float8_e5m2).view(np.uint8)
    else:
        c = by_word.astype(ml_dtypes.float4_e2m1fn).view(np.uint8) & 0xF
        words = (c[..., 0::2] | (c[..., 1::2] << 4)).reshape(k // 512, 128, 2 * n)
    return np.ascontiguousarray(words), np.ascontiguousarray(byte.astype(np.uint8).reshape(k // 512, 16, n))


def unpack_weight(words, scales, fmt):
    g, _, n = scales.shape
    words = np.ascontiguousarray(words).reshape(g, 128, n, -1)
    if fmt in ("e4m3", "e5m2"):
        vals = words.view(ml_dtypes.float8_e4m3fn if fmt == "e4m3" else ml_dtypes.float8_e5m2).astype(np.float64)
    else:
        nib = np.empty((g, 128, n, 4), np.uint8)
        nib[..., 0::2] = words & 0xF
        nib[..., 1::2] = words >> 4
        vals = E2M1[nib]
    vals = vals * np.repeat(np.exp2(scales.astype(np.float64) - 127.0), 8, axis=1)[..., None]
    return vals.transpose(0, 1, 3, 2).reshape(g * 512, n)


K, T, J, R, V, C, O, U, D, N, E = 512, 1024, 256, 512, 1024, 512, 128, 128, 256, 256, 512


def setup_inputs():
    n = np.random.standard_normal
    idx = np.random.permutation(V)[:R]
    idx2 = np.random.permutation(T)[:J]
    idx3 = np.stack([np.random.permutation(C)[:J] for _ in range(8)])
    idx4 = np.random.permutation(C)[:O]
    idx5 = np.random.permutation(C)[:U]
    idx6 = np.stack([np.random.permutation(E)[:D] for _ in range(8)])
    fk = mx_kscale(K)
    fr = mx_kscale(R)
    tr = np.ones(V)
    tr[idx] = fr
    xtp = pack_weight(n((K, T)) / fk[:, None], "e4m3")
    wtp = pack_weight(n((K, V)) * 1 / np.sqrt(K) * fk[:, None] * tr, "e2m1")
    wbp = pack_weight(n((R, N)) * 1 / np.sqrt(R) / fr[:, None], "e5m2")
    return {
        "xt_words": xtp[0],
        "xt_scales": xtp[1],
        "wt_words": wtp[0],
        "wt_scales": wtp[1],
        "sa": (np.random.uniform(0.5, 1.6, (R, 1))).astype(np.float32),
        "sb": (np.random.uniform(0.5, 1.6, (R, 1))).astype(np.float32),
        "wb_words": wbp[0],
        "wb_scales": wbp[1],
        "offs": striped(idx),
        "offs2": striped(idx2),
        "offs3": striped8(idx3),
        "offs4": striped(idx4),
        "offs5": striped(idx5),
        "offs6": striped8(idx6),
    }


def reference(xt_words, xt_scales, wt_words, wt_scales, sa, sb, wb_words, wb_scales, offs, offs2, offs3, offs4, offs5, offs6):
    idx = unstriped(offs)
    idx2 = unstriped(offs2)
    idx3 = unstriped8(offs3)
    idx4 = unstriped(offs4)
    idx5 = unstriped(offs5)
    idx6 = unstriped8(offs6)
    xtu = unpack_weight(xt_words, xt_scales, "e4m3")
    wtu = unpack_weight(wt_words, wt_scales, "e2m1")
    wbu = unpack_weight(wb_words, wb_scales, "e5m2")
    wtidxg = wtu[:, idx]
    xtidx2g = xtu[:, idx2]
    a = wtidxg.T @ xtidx2g
    pw = np.zeros((R, C))
    pw[np.arange(R)[:, None], idx3[np.arange(R) % 512 // 64]] = a
    h1 = pw[:, idx4] * f64(sa)
    h2 = pw[:, idx5] * f64(sb)
    hid = np.concatenate([h1, h2], axis=1)
    hidq = mxq(hid, 0, "e4m3")
    p = wbu.T @ hidq
    y = np.zeros((N, E))
    y[np.arange(N)[:, None], idx6[np.arange(N) % 128 // 16]] = p
    return y

@@ -1,0 +1,163 @@
+from contextlib import ExitStack
+
+import concourse.mybir as mybir
+
+F32 = mybir.dt.float32
+BF16 = mybir.dt.bfloat16
+I32 = mybir.dt.int32
+U32 = mybir.dt.uint32
+U16 = mybir.dt.uint16
+U8 = mybir.dt.uint8
+E4M3 = mybir.dt.float8_e4m3fn_x4
+E5M2 = mybir.dt.float8_e5m2_x4
+E2M1 = mybir.dt.float4_e2m1fn_x4
+COPY = mybir.ActivationFunctionType.Copy
+
+K, T, J, R, V, C, O, U, D, N, E = 512, 1024, 256, 512, 1024, 512, 128, 128, 256, 256, 512
+P = 128
+PACK = 4
+HALF = 128
+LIST_COLS = HALF // 16
+
+FLOPS = 2 * K * R * J + 2 * R * N * D
+
+
+def tile_list_ownsides_chosen_one_ownpage_kernel(
+    tc, xt_words, xt_scales, wt_words, wt_scales, sa, sb, wb_words, wb_scales,
+    offs, offs2, offs3, offs4, offs5, offs6, out,
+):
+    nc = tc.nc
+    with ExitStack() as ctx:
+        lists = ctx.enter_context(tc.tile_pool(name="lists", bufs=1))
+        pool = ctx.enter_context(tc.tile_pool(name="held", bufs=1))
+        psum = ctx.enter_context(tc.psum_pool(name="psum", bufs=1))
+
+        def tile(shape, dtype, name, tag=None, bufs=1):
+            return pool.tile(shape, dtype, name=name, tag=tag or name, bufs=bufs, align_bytes=64)
+
+        def load_list(src, name):
+            dst = lists.tile(list(src.shape), U16, name=name)
+            nc.sync.dma_start(dst[:], src)
+            return dst
+
+        def load_scale_rows(queue, plane, scales):
+            for q in range(4):
+                queue.dma_start(plane[32 * q : 32 * q + 4, :].bitcast(I32), scales[0, 4 * q : 4 * q + 4, :].bitcast(I32))
+
+        wt_plane = tile([P, V], U8, "wt_plane")
+        xt_plane = tile([P, T], U8, "xt_plane")
+        wb_plane = tile([P, N], U8, "wb_plane")
+        nc.vector.memset(wt_plane[:].bitcast(I32), 0)
+        nc.vector.memset(xt_plane[:].bitcast(I32), 0)
+        nc.gpsimd.memset(wb_plane[:].bitcast(I32), 0)
+
+        list_r = load_list(offs, "list_r")
+        list_j = load_list(offs2, "list_j")
+        list_board = load_list(offs3, "list_board")
+        list_o = load_list(offs4, "list_o")
+        wt_table = tile([P, V], U16, "wt_table")
+        nc.sync.dma_start(wt_table[:].bitcast(I32), wt_words[0].bitcast(I32))
+        list_u = load_list(offs5, "list_u")
+        list_page = load_list(offs6, "list_page")
+        xt_table = tile([P, T], U32, "xt_table")
+        nc.sync.dma_start(xt_table[:].bitcast(I32), xt_words[0].rearrange("p n t -> p (n t)").bitcast(I32))
+        load_scale_rows(nc.sync, wt_plane, wt_scales)
+        load_scale_rows(nc.sync, xt_plane, xt_scales)
+        sa_sb = tile([P, PACK], F32, "sa_sb")
+        nc.gpsimd.dma_start(sa_sb[:], sa.rearrange("(p t) o -> p (t o)", t=PACK))
+        sb_sb = tile([P, PACK], F32, "sb_sb")
+        nc.gpsimd.dma_start(sb_sb[:], sb.rearrange("(p t) o -> p (t o)", t=PACK))
+        wb_codes = tile([P, N], U32, "wb_codes")
+        nc.gpsimd.dma_start(wb_codes[:].bitcast(I32), wb_words[0].rearrange("p n t -> p (n t)").bitcast(I32))
+        load_scale_rows(nc.gpsimd, wb_plane, wb_scales)
+
+        board = [tile([P, C], F32, "board%d" % t) for t in range(PACK)]
+        for t in range(PACK):
+            nc.vector.memset(board[t][:], 0.0)
+
+        w_words = tile([P, R], U16, "w_words")
+        w_bytes = tile([P, R], U8, "w_bytes")
+        x_words = tile([P, J], U32, "x_words")
+        x_bytes = tile([P, J], U8, "x_bytes")
+
+        def gather_x(h):
+            cols = slice(HALF * h, HALF * (h + 1))
+            part = list_j[:, LIST_COLS * h : LIST_COLS * (h + 1)]
+            nc.vector.tensor_copy(x_words[:, cols], xt_table[:].indirect(part))
+            nc.vector.tensor_copy(x_bytes[:, cols], xt_plane[:].indirect(part))
+
+        dealt_words = {}
+        dealt_bytes = {}
+
+        def deal_words(t):
+            dealt_words[t] = tile([P, P], U16, "dealt_words%d" % t, tag="dealt_words", bufs=2)
+            nc.vector.tensor_copy(dealt_words[t][:], w_words[:, t::PACK])
+
+        def deal_bytes(t):
+            dealt_bytes[t] = tile([P, P], U8, "dealt_bytes%d" % t, tag="dealt_bytes", bufs=2)
+            nc.vector.tensor_copy(dealt_bytes[t][:], w_bytes[:, t::PACK])
+
+        def first_product(t, lo, hi):
+            acc = psum.tile([P, hi - lo], F32, name="a_acc%d_%d" % (t, lo))
+            nc.tensor.matmul_mx(
+                acc[:], lhsT=dealt_words[t][:].bitcast(E2M1), lhsT_scale=dealt_bytes[t][:],
+                rhs=x_words[:, lo:hi].bitcast(E4M3), rhs_scale=x_bytes[:, lo:hi], start=True, stop=True,
+            )
+            rows = tile([P, hi - lo], F32, "a_rows%d_%d" % (t, lo))
+            nc.vector.tensor_copy(rows[:], acc[:])
+            return rows
+
+        def put(t, lo, hi, rows):
+            nc.scalar.activation(board[t][:].indirect(list_board[:, lo // 16 : hi // 16]), rows[:], COPY)
+
+        picked = [tile([P, PACK, HALF], BF16, "picked%d" % h) for h in range(2)]
+
+        def pick(h, t):
+            places, weight = ((list_o, sa_sb), (list_u, sb_sb))[h]
+            nc.scalar.activation(picked[h][:, t, :], board[t][:].indirect(places[:]), COPY, scale=weight[:, t : t + 1])
+
+        nc.vector.tensor_copy(w_words[:], wt_table[:].indirect(list_r[:]))
+        deal_words(0)
+        nc.vector.tensor_copy(w_bytes[:], wt_plane[:].indirect(list_r[:]))
+        gather_x(0)
+        deal_bytes(0)
+        deal_words(1)
+        deal_bytes(1)
+        for t in range(2):
+            put(t, 0, HALF, first_product(t, 0, HALF))
+        gather_x(1)
+        for t in range(2):
+            put(t, HALF, J, first_product(t, HALF, J))
+        for t in range(2, PACK):
+            deal_words(t)
+            deal_bytes(t)
+        for t in range(2, PACK):
+            pick(0, t - 2)
+            put(t, 0, J, first_product(t, 0, J))
+        for t in range(2, PACK):
+            pick(0, t)
+        for t in range(PACK):
+            pick(1, t)
+
+        page = [tile([P, E], F32, "page%d" % b, tag="a_rows%d_%d" % (b, HALF)) for b in range(N // P)]
+        for b in range(N // P):
+            nc.vector.memset(page[b][:], 0.0)
+
+        for h in range(2):
+            woven = tile([P, HALF, PACK], BF16, "woven%d" % h)
+            nc.vector.tensor_copy(woven[:], picked[h][:].rearrange("p t d -> p d t"))
+            hid_words = tile([P, HALF], U32, "hid_words%d" % h)
+            hid_bytes = tile([P, HALF], U8, "hid_bytes%d" % h)
+            nc.vector.quantize_mx(hid_words[:].bitcast(E4M3), hid_bytes[:], woven[:].rearrange("p d t -> p (d t)"))
+            acc = psum.tile([P, N // P, HALF], F32, name="p_acc%d" % h)
+            for b in range(N // P):
+                nc.tensor.matmul_mx(
+                    acc[:, b, :], lhsT=wb_codes[:, P * b : P * (b + 1)].bitcast(E5M2), lhsT_scale=wb_plane[:, P * b : P * (b + 1)],
+                    rhs=hid_words[:].bitcast(E4M3), rhs_scale=hid_bytes[:], start=True, stop=True,
+                )
+            for b in range(N // P):
+                rows = tile([P, HALF], F32, "p_rows%d_%d" % (h, b))
+                nc.vector.tensor_copy(rows[:], acc[:, b, :])
+                nc.scalar.activation(page[b][:].indirect(list_page[:, LIST_COLS * h : LIST_COLS * (h + 1)]), rows[:], COPY)
+        for b in range(N // P):
+            nc.sync.dma_start(out[P * b : P * (b + 1), :], page[b][:])

@@ -52,24 +52,24 @@ def tile_list_ownsides_chosen_one_ownpage_kernel(
         nc.gpsimd.memset(wb_plane[:].bitcast(I32), 0)
 
         list_r = load_list(offs, "list_r")
-        list_j = load_list(offs2, "list_j")
-        list_board = load_list(offs3, "list_board")
-        list_o = load_list(offs4, "list_o")
         wt_table = tile([P, V], U16, "wt_table")
         nc.sync.dma_start(wt_table[:].bitcast(I32), wt_words[0].bitcast(I32))
-        list_u = load_list(offs5, "list_u")
-        list_page = load_list(offs6, "list_page")
+        load_scale_rows(nc.sync, wt_plane, wt_scales)
+        list_j = load_list(offs2, "list_j")
         xt_table = tile([P, T], U32, "xt_table")
         nc.sync.dma_start(xt_table[:].bitcast(I32), xt_words[0].rearrange("p n t -> p (n t)").bitcast(I32))
-        load_scale_rows(nc.sync, wt_plane, wt_scales)
         load_scale_rows(nc.sync, xt_plane, xt_scales)
+        list_board = load_list(offs3, "list_board")
+        list_o = load_list(offs4, "list_o")
+        list_u = load_list(offs5, "list_u")
+        list_page = load_list(offs6, "list_page")
         sa_sb = tile([P, PACK], F32, "sa_sb")
-        nc.gpsimd.dma_start(sa_sb[:], sa.rearrange("(p t) o -> p (t o)", t=PACK))
+        nc.sync.dma_start(sa_sb[:], sa.rearrange("(p t) o -> p (t o)", t=PACK))
         sb_sb = tile([P, PACK], F32, "sb_sb")
-        nc.gpsimd.dma_start(sb_sb[:], sb.rearrange("(p t) o -> p (t o)", t=PACK))
+        nc.sync.dma_start(sb_sb[:], sb.rearrange("(p t) o -> p (t o)", t=PACK))
         wb_codes = tile([P, N], U32, "wb_codes")
-        nc.gpsimd.dma_start(wb_codes[:].bitcast(I32), wb_words[0].rearrange("p n t -> p (n t)").bitcast(I32))
-        load_scale_rows(nc.gpsimd, wb_plane, wb_scales)
+        nc.sync.dma_start(wb_codes[:].bitcast(I32), wb_words[0].rearrange("p n t -> p (n t)").bitcast(I32))
+        load_scale_rows(nc.sync, wb_plane, wb_scales)
 
         board = [tile([P, C], F32, "board%d" % t) for t in range(PACK)]
         for t in range(PACK):
@@ -77,87 +77,109 @@ def tile_list_ownsides_chosen_one_ownpage_kernel(
 
         w_words = tile([P, R], U16, "w_words")
         w_bytes = tile([P, R], U8, "w_bytes")
-        x_words = tile([P, J], U32, "x_words")
-        x_bytes = tile([P, J], U8, "x_bytes")
 
-        def gather_x(h):
-            cols = slice(HALF * h, HALF * (h + 1))
-            part = list_j[:, LIST_COLS * h : LIST_COLS * (h + 1)]
-            nc.vector.tensor_copy(x_words[:, cols], xt_table[:].indirect(part))
-            nc.vector.tensor_copy(x_bytes[:, cols], xt_plane[:].indirect(part))
+        def slots(h):
+            return list_j[:, LIST_COLS * h : LIST_COLS * (h + 1)]
 
-        dealt_words = {}
-        dealt_bytes = {}
+        def deal(gathered, dtype, pair, name):
+            dealt = tile([P, 2, P], dtype, name)
+            nc.vector.tensor_copy(dealt[:], gathered[:].rearrange("p (m t) -> p t m", t=PACK)[:, 2 * pair : 2 * pair + 2, :])
+            return dealt
 
-        def deal_words(t):
-            dealt_words[t] = tile([P, P], U16, "dealt_words%d" % t, tag="dealt_words", bufs=2)
-            nc.vector.tensor_copy(dealt_words[t][:], w_words[:, t::PACK])
-
-        def deal_bytes(t):
-            dealt_bytes[t] = tile([P, P], U8, "dealt_bytes%d" % t, tag="dealt_bytes", bufs=2)
-            nc.vector.tensor_copy(dealt_bytes[t][:], w_bytes[:, t::PACK])
-
-        def first_product(t, lo, hi):
-            acc = psum.tile([P, hi - lo], F32, name="a_acc%d_%d" % (t, lo))
+        def product(acc, words, scale_bytes, i, x_words, x_bytes):
             nc.tensor.matmul_mx(
-                acc[:], lhsT=dealt_words[t][:].bitcast(E2M1), lhsT_scale=dealt_bytes[t][:],
-                rhs=x_words[:, lo:hi].bitcast(E4M3), rhs_scale=x_bytes[:, lo:hi], start=True, stop=True,
+                acc, lhsT=words[:, i, :].bitcast(E2M1), lhsT_scale=scale_bytes[:, i, :],
+                rhs=x_words[:].bitcast(E4M3), rhs_scale=x_bytes[:], start=True, stop=True,
             )
-            rows = tile([P, hi - lo], F32, "a_rows%d_%d" % (t, lo))
-            nc.vector.tensor_copy(rows[:], acc[:])
+
+        def put(t, h, rows):
+            nc.scalar.activation(board[t][:].indirect(list_board[:, LIST_COLS * h : LIST_COLS * (h + 1)]), rows[:], COPY)
+
+        def pick(picked, t, places, weight):
+            nc.scalar.activation(picked[:, t, :], board[t][:].indirect(places[:]), COPY, scale=weight[:, t : t + 1])
+
+        def pair_of_rows(pair, h, words, scale_bytes, x_words, x_bytes):
+            acc = psum.tile([P, 2, HALF], F32, name="a_acc%d_%d" % (pair, h))
+            rows = []
+            for i in range(2):
+                product(acc[:, i, :], words, scale_bytes, i, x_words, x_bytes)
+            for i in range(2):
+                rows.append(tile([P, HALF], F32, "a_rows%d_%d" % (2 * pair + i, h)))
+                nc.vector.tensor_copy(rows[i][:], acc[:, i, :])
             return rows
 
-        def put(t, lo, hi, rows):
-            nc.scalar.activation(board[t][:].indirect(list_board[:, lo // 16 : hi // 16]), rows[:], COPY)
-
-        picked = [tile([P, PACK, HALF], BF16, "picked%d" % h) for h in range(2)]
-
-        def pick(h, t):
-            places, weight = ((list_o, sa_sb), (list_u, sb_sb))[h]
-            nc.scalar.activation(picked[h][:, t, :], board[t][:].indirect(places[:]), COPY, scale=weight[:, t : t + 1])
-
         nc.vector.tensor_copy(w_words[:], wt_table[:].indirect(list_r[:]))
-        deal_words(0)
+        words = deal(w_words, U16, 0, "dealt_words")
         nc.vector.tensor_copy(w_bytes[:], wt_plane[:].indirect(list_r[:]))
-        gather_x(0)
-        deal_bytes(0)
-        deal_words(1)
-        deal_bytes(1)
+        scale_bytes = deal(w_bytes, U8, 0, "dealt_bytes")
+        x_words0 = tile([P, HALF], U32, "x_words0")
+        x_bytes0 = tile([P, HALF], U8, "x_bytes0")
+        nc.vector.tensor_copy(x_words0[:], xt_table[:].indirect(slots(0)))
+        nc.vector.tensor_copy(x_bytes0[:], xt_plane[:].indirect(slots(0)))
         for t in range(2):
-            put(t, 0, HALF, first_product(t, 0, HALF))
-        gather_x(1)
-        for t in range(2):
-            put(t, HALF, J, first_product(t, HALF, J))
-        for t in range(2, PACK):
-            deal_words(t)
-            deal_bytes(t)
-        for t in range(2, PACK):
-            pick(0, t - 2)
-            put(t, 0, J, first_product(t, 0, J))
-        for t in range(2, PACK):
-            pick(0, t)
-        for t in range(PACK):
-            pick(1, t)
+            acc = psum.tile([P, HALF], F32, name="a_first%d" % t)
+            product(acc[:], words, scale_bytes, t, x_words0, x_bytes0)
+            rows = tile([P, HALF], F32, "a_rows%d_0" % t)
+            if t == 0:
+                nc.scalar.copy(rows[:], acc[:])
+            else:
+                nc.vector.tensor_copy(rows[:], acc[:])
+            put(t, 0, rows)
 
-        page = [tile([P, E], F32, "page%d" % b, tag="a_rows%d_%d" % (b, HALF)) for b in range(N // P)]
+        words = deal(w_words, U16, 1, "dealt_words")
+        scale_bytes = deal(w_bytes, U8, 1, "dealt_bytes")
+        rows = pair_of_rows(1, 0, words, scale_bytes, x_words0, x_bytes0)
+        put(2, 0, rows[0])
+        put(3, 0, rows[1])
+
+        x_words1 = tile([P, HALF], U32, "x_words1", tag="x_words0")
+        x_bytes1 = tile([P, HALF], U8, "x_bytes1", tag="x_bytes0")
+        nc.vector.tensor_copy(x_words1[:], xt_table[:].indirect(slots(1)))
+        nc.vector.tensor_copy(x_bytes1[:], xt_plane[:].indirect(slots(1)))
+        rows = pair_of_rows(1, 1, words, scale_bytes, x_words1, x_bytes1)
+        put(2, 1, rows[0])
+        put(3, 1, rows[1])
+
+        words = deal(w_words, U16, 0, "dealt_words")
+        scale_bytes = deal(w_bytes, U8, 0, "dealt_bytes")
+        rows = pair_of_rows(0, 1, words, scale_bytes, x_words1, x_bytes1)
+        picked = [tile([P, PACK, HALF], BF16, "picked0")]
+        put(0, 1, rows[0])
+        pick(picked[0], 2, list_o, sa_sb)
+        put(1, 1, rows[1])
+        for t in (3, 0, 1):
+            pick(picked[0], t, list_o, sa_sb)
+        picked.append(tile([P, PACK, HALF], BF16, "picked1", tag="sa_sb"))
+        for t in (2, 3, 0, 1):
+            pick(picked[1], t, list_u, sb_sb)
+
+        page = [tile([P, E], F32, "page%d" % b, tag="a_rows%d_1" % b) for b in range(N // P)]
         for b in range(N // P):
             nc.vector.memset(page[b][:], 0.0)
 
         for h in range(2):
-            woven = tile([P, HALF, PACK], BF16, "woven%d" % h)
-            nc.vector.tensor_copy(woven[:], picked[h][:].rearrange("p t d -> p d t"))
-            hid_words = tile([P, HALF], U32, "hid_words%d" % h)
+            woven = tile([P, HALF, PACK], BF16, "woven%d" % h, tag="woven")
+            for lo in (2, 0):
+                nc.vector.tensor_copy(woven[:, :, lo : lo + 2], picked[h][:, lo : lo + 2, :].rearrange("p t d -> p d t"))
+            hid_words = tile([P, HALF], U32, "hid_words%d" % h, tag="hid_words")
             hid_bytes = tile([P, HALF], U8, "hid_bytes%d" % h)
             nc.vector.quantize_mx(hid_words[:].bitcast(E4M3), hid_bytes[:], woven[:].rearrange("p d t -> p (d t)"))
-            acc = psum.tile([P, N // P, HALF], F32, name="p_acc%d" % h)
+            if h == 0:
+                accs = [psum.tile([P, HALF], F32, name="p_first%d" % b)[:] for b in range(N // P)]
+            else:
+                both = psum.tile([P, N // P, HALF], F32, name="p_second")
+                accs = [both[:, b, :] for b in range(N // P)]
             for b in range(N // P):
                 nc.tensor.matmul_mx(
-                    acc[:, b, :], lhsT=wb_codes[:, P * b : P * (b + 1)].bitcast(E5M2), lhsT_scale=wb_plane[:, P * b : P * (b + 1)],
+                    accs[b], lhsT=wb_codes[:, P * b : P * (b + 1)].bitcast(E5M2), lhsT_scale=wb_plane[:, P * b : P * (b + 1)],
                     rhs=hid_words[:].bitcast(E4M3), rhs_scale=hid_bytes[:], start=True, stop=True,
                 )
             for b in range(N // P):
                 rows = tile([P, HALF], F32, "p_rows%d_%d" % (h, b))
-                nc.vector.tensor_copy(rows[:], acc[:, b, :])
+                if h == 0 and b == 0:
+                    nc.scalar.copy(rows[:], accs[b])
+                else:
+                    nc.vector.tensor_copy(rows[:], accs[b])
                 nc.scalar.activation(page[b][:].indirect(list_page[:, LIST_COLS * h : LIST_COLS * (h + 1)]), rows[:], COPY)
         for b in range(N // P):
             nc.sync.dma_start(out[P * b : P * (b + 1), :], page[b][:])

@@ -30,6 +30,7 @@ def tile_list_ownsides_chosen_one_ownpage_kernel(
     with ExitStack() as ctx:
         lists = ctx.enter_context(tc.tile_pool(name="lists", bufs=1))
         pool = ctx.enter_context(tc.tile_pool(name="held", bufs=1))
+        reused = ctx.enter_context(tc.tile_pool(name="reused", bufs=1))
         psum = ctx.enter_context(tc.psum_pool(name="psum", bufs=1))
 
         def tile(shape, dtype, name, tag=None, bufs=1):
@@ -44,21 +45,21 @@ def tile_list_ownsides_chosen_one_ownpage_kernel(
             for q in range(4):
                 queue.dma_start(plane[32 * q : 32 * q + 4, :].bitcast(I32), scales[0, 4 * q : 4 * q + 4, :].bitcast(I32))
 
-        wt_plane = tile([P, V], U8, "wt_plane")
+        wt_plane = reused.tile([P, V], U8, name="wt_plane", align_bytes=64, offset=0)
         xt_plane = tile([P, T], U8, "xt_plane")
         wb_plane = tile([P, N], U8, "wb_plane")
-        nc.vector.memset(wt_plane[:].bitcast(I32), 0)
         nc.vector.memset(xt_plane[:].bitcast(I32), 0)
+        nc.vector.memset(wt_plane[:].bitcast(I32), 0)
         nc.gpsimd.memset(wb_plane[:].bitcast(I32), 0)
 
         list_r = load_list(offs, "list_r")
+        list_j = load_list(offs2, "list_j")
         wt_table = tile([P, V], U16, "wt_table")
         nc.sync.dma_start(wt_table[:].bitcast(I32), wt_words[0].bitcast(I32))
-        load_scale_rows(nc.sync, wt_plane, wt_scales)
-        list_j = load_list(offs2, "list_j")
+        load_scale_rows(nc.sync, xt_plane, xt_scales)
         xt_table = tile([P, T], U32, "xt_table")
         nc.sync.dma_start(xt_table[:].bitcast(I32), xt_words[0].rearrange("p n t -> p (n t)").bitcast(I32))
-        load_scale_rows(nc.sync, xt_plane, xt_scales)
+        load_scale_rows(nc.sync, wt_plane, wt_scales)
         list_board = load_list(offs3, "list_board")
         list_o = load_list(offs4, "list_o")
         list_u = load_list(offs5, "list_u")
@@ -81,85 +82,75 @@ def tile_list_ownsides_chosen_one_ownpage_kernel(
         def slots(h):
             return list_j[:, LIST_COLS * h : LIST_COLS * (h + 1)]
 
-        def deal(gathered, dtype, pair, name):
-            dealt = tile([P, 2, P], dtype, name)
-            nc.vector.tensor_copy(dealt[:], gathered[:].rearrange("p (m t) -> p t m", t=PACK)[:, 2 * pair : 2 * pair + 2, :])
-            return dealt
+        def deal(gathered, dealt, lo, hi):
+            nc.vector.tensor_copy(dealt, gathered[:].rearrange("p (m t) -> p t m", t=PACK)[:, lo:hi, :])
 
-        def product(acc, words, scale_bytes, i, x_words, x_bytes):
+        def product(acc, t, h):
             nc.tensor.matmul_mx(
-                acc, lhsT=words[:, i, :].bitcast(E2M1), lhsT_scale=scale_bytes[:, i, :],
-                rhs=x_words[:].bitcast(E4M3), rhs_scale=x_bytes[:], start=True, stop=True,
+                acc, lhsT=words[t // 2][:, t % 2, :].bitcast(E2M1), lhsT_scale=scale_bytes[:, t, :],
+                rhs=x_words[h][:].bitcast(E4M3), rhs_scale=x_bytes[h][:], start=True, stop=True,
             )
 
         def put(t, h, rows):
-            nc.scalar.activation(board[t][:].indirect(list_board[:, LIST_COLS * h : LIST_COLS * (h + 1)]), rows[:], COPY)
+            nc.scalar.activation(board[t][:].indirect(list_board[:, LIST_COLS * h : LIST_COLS * (h + 1)]), rows, COPY)
 
         def pick(picked, t, places, weight):
             nc.scalar.activation(picked[:, t, :], board[t][:].indirect(places[:]), COPY, scale=weight[:, t : t + 1])
 
-        def pair_of_rows(pair, h, words, scale_bytes, x_words, x_bytes):
-            acc = psum.tile([P, 2, HALF], F32, name="a_acc%d_%d" % (pair, h))
-            rows = []
-            for i in range(2):
-                product(acc[:, i, :], words, scale_bytes, i, x_words, x_bytes)
-            for i in range(2):
-                rows.append(tile([P, HALF], F32, "a_rows%d_%d" % (2 * pair + i, h)))
-                nc.vector.tensor_copy(rows[i][:], acc[:, i, :])
-            return rows
-
+        x_words = [tile([P, HALF], U32, "x_words0"), reused.tile([P, HALF], U32, name="x_words1", align_bytes=64, offset=0)]
+        x_bytes = [tile([P, HALF], U8, "x_bytes0"), reused.tile([P, HALF], U8, name="x_bytes1", align_bytes=64, offset=4 * HALF)]
+        words = [tile([P, 2, P], U16, "dealt_words0"), reused.tile([P, 2, P], U16, name="dealt_words1", align_bytes=64, offset=5 * HALF)]
+        scale_bytes = tile([P, PACK, P], U8, "dealt_bytes")
         nc.vector.tensor_copy(w_words[:], wt_table[:].indirect(list_r[:]))
-        words = deal(w_words, U16, 0, "dealt_words")
+        deal(w_words, words[0][:], 0, 2)
+        nc.vector.tensor_copy(x_bytes[0][:], xt_plane[:].indirect(slots(0)))
+        nc.vector.tensor_copy(x_words[0][:], xt_table[:].indirect(slots(0)))
         nc.vector.tensor_copy(w_bytes[:], wt_plane[:].indirect(list_r[:]))
-        scale_bytes = deal(w_bytes, U8, 0, "dealt_bytes")
-        x_words0 = tile([P, HALF], U32, "x_words0")
-        x_bytes0 = tile([P, HALF], U8, "x_bytes0")
-        nc.vector.tensor_copy(x_words0[:], xt_table[:].indirect(slots(0)))
-        nc.vector.tensor_copy(x_bytes0[:], xt_plane[:].indirect(slots(0)))
+        for t in range(2):
+            deal(w_bytes, scale_bytes[:, t : t + 1, :], t, t + 1)
         for t in range(2):
             acc = psum.tile([P, HALF], F32, name="a_first%d" % t)
-            product(acc[:], words, scale_bytes, t, x_words0, x_bytes0)
-            rows = tile([P, HALF], F32, "a_rows%d_0" % t)
+            product(acc[:], t, 0)
+            rows = tile([P, HALF], F32, "a_rows%d" % t)
             if t == 0:
                 nc.scalar.copy(rows[:], acc[:])
             else:
                 nc.vector.tensor_copy(rows[:], acc[:])
-            put(t, 0, rows)
+            put(t, 0, rows[:])
 
-        words = deal(w_words, U16, 1, "dealt_words")
-        scale_bytes = deal(w_bytes, U8, 1, "dealt_bytes")
-        rows = pair_of_rows(1, 0, words, scale_bytes, x_words0, x_bytes0)
-        put(2, 0, rows[0])
-        put(3, 0, rows[1])
+        deal(w_words, words[1][:], 2, 4)
+        deal(w_bytes, scale_bytes[:, 2:4, :], 2, 4)
+        acc = psum.tile([P, 2, HALF], F32, name="a_second")
+        for t in range(2, PACK):
+            product(acc[:, t - 2, :], t, 0)
+        rows = tile([P, 2, HALF], F32, "a_rows_second")
+        nc.vector.tensor_copy(rows[:], acc[:])
+        for t in range(2, PACK):
+            put(t, 0, rows[:, t - 2, :])
 
-        x_words1 = tile([P, HALF], U32, "x_words1", tag="x_words0")
-        x_bytes1 = tile([P, HALF], U8, "x_bytes1", tag="x_bytes0")
-        nc.vector.tensor_copy(x_words1[:], xt_table[:].indirect(slots(1)))
-        nc.vector.tensor_copy(x_bytes1[:], xt_plane[:].indirect(slots(1)))
-        rows = pair_of_rows(1, 1, words, scale_bytes, x_words1, x_bytes1)
-        put(2, 1, rows[0])
-        put(3, 1, rows[1])
-
-        words = deal(w_words, U16, 0, "dealt_words")
-        scale_bytes = deal(w_bytes, U8, 0, "dealt_bytes")
-        rows = pair_of_rows(0, 1, words, scale_bytes, x_words1, x_bytes1)
+        nc.vector.tensor_copy(x_words[1][:], xt_table[:].indirect(slots(1)))
+        nc.vector.tensor_copy(x_bytes[1][:], xt_plane[:].indirect(slots(1)))
+        acc = psum.tile([P, PACK, HALF], F32, name="a_third")
+        for t in range(PACK):
+            product(acc[:, t, :], t, 1)
+        rows = tile([P, PACK, HALF], F32, "a_rows_third")
+        nc.vector.tensor_copy(rows[:], acc[:])
+        for t in range(PACK):
+            put(t, 1, rows[:, t, :])
         picked = [tile([P, PACK, HALF], BF16, "picked0")]
-        put(0, 1, rows[0])
-        pick(picked[0], 2, list_o, sa_sb)
-        put(1, 1, rows[1])
-        for t in (3, 0, 1):
+        for t in range(PACK):
             pick(picked[0], t, list_o, sa_sb)
         picked.append(tile([P, PACK, HALF], BF16, "picked1", tag="sa_sb"))
-        for t in (2, 3, 0, 1):
+        for t in range(PACK):
             pick(picked[1], t, list_u, sb_sb)
 
-        page = [tile([P, E], F32, "page%d" % b, tag="a_rows%d_1" % b) for b in range(N // P)]
+        page = [tile([P, E], F32, "page%d" % b, tag=("dealt_words0", "dealt_bytes")[b]) for b in range(N // P)]
         for b in range(N // P):
             nc.vector.memset(page[b][:], 0.0)
 
         for h in range(2):
             woven = tile([P, HALF, PACK], BF16, "woven%d" % h, tag="woven")
-            for lo in (2, 0):
+            for lo in (0, 2):
                 nc.vector.tensor_copy(woven[:, :, lo : lo + 2], picked[h][:, lo : lo + 2, :].rearrange("p t d -> p d t"))
             hid_words = tile([P, HALF], U32, "hid_words%d" % h, tag="hid_words")
             hid_bytes = tile([P, HALF], U8, "hid_bytes%d" % h)

@@ -77,7 +77,6 @@ def tile_list_ownsides_chosen_one_ownpage_kernel(
             nc.vector.memset(board[t][:], 0.0)
 
         w_words = tile([P, R], U16, "w_words")
-        w_bytes = tile([P, R], U8, "w_bytes")
 
         def slots(h):
             return list_j[:, LIST_COLS * h : LIST_COLS * (h + 1)]
@@ -105,9 +104,7 @@ def tile_list_ownsides_chosen_one_ownpage_kernel(
         deal(w_words, words[0][:], 0, 2)
         nc.vector.tensor_copy(x_bytes[0][:], xt_plane[:].indirect(slots(0)))
         nc.vector.tensor_copy(x_words[0][:], xt_table[:].indirect(slots(0)))
-        nc.vector.tensor_copy(w_bytes[:], wt_plane[:].indirect(list_r[:]))
-        for t in range(2):
-            deal(w_bytes, scale_bytes[:, t : t + 1, :], t, t + 1)
+        nc.vector.tensor_copy(scale_bytes[:].rearrange("p t m -> p m t"), wt_plane[:].indirect(list_r[:]))
         for t in range(2):
             acc = psum.tile([P, HALF], F32, name="a_first%d" % t)
             product(acc[:], t, 0)
@@ -119,7 +116,6 @@ def tile_list_ownsides_chosen_one_ownpage_kernel(
             put(t, 0, rows[:])
 
         deal(w_words, words[1][:], 2, 4)
-        deal(w_bytes, scale_bytes[:, 2:4, :], 2, 4)
         acc = psum.tile([P, 2, HALF], F32, name="a_second")
         for t in range(2, PACK):
             product(acc[:, t - 2, :], t, 0)

@@ -13,11 +13,14 @@ E5M2 = mybir.dt.float8_e5m2_x4
 E2M1 = mybir.dt.float4_e2m1fn_x4
 COPY = mybir.ActivationFunctionType.Copy
 
-K, T, J, R, V, C, O, U, D, N, E = 512, 1024, 256, 512, 1024, 512, 128, 128, 256, 256, 512
+K, T, J, R, V, C, D, N, E = 512, 1024, 256, 512, 1024, 512, 256, 256, 512
 P = 128
 PACK = 4
+PAIR = 2
 HALF = 128
-LIST_COLS = HALF // 16
+HALF_COLS = HALF // 16
+QUADRANTS = 4
+ALIGN = 64
 
 FLOPS = 2 * K * R * J + 2 * R * N * D
 
@@ -33,19 +36,25 @@ def tile_list_ownsides_chosen_one_ownpage_kernel(
         reused = ctx.enter_context(tc.tile_pool(name="reused", bufs=1))
         psum = ctx.enter_context(tc.psum_pool(name="psum", bufs=1))
 
-        def tile(shape, dtype, name, tag=None, bufs=1):
-            return pool.tile(shape, dtype, name=name, tag=tag or name, bufs=bufs, align_bytes=64)
+        def tile(shape, dtype, name, tag=None):
+            return pool.tile(shape, dtype, name=name, tag=tag or name, bufs=1, align_bytes=ALIGN)
+
+        def after_wt_plane(shape, dtype, name, offset):
+            return reused.tile(shape, dtype, name=name, align_bytes=ALIGN, offset=offset)
 
         def load_list(src, name):
             dst = lists.tile(list(src.shape), U16, name=name)
             nc.sync.dma_start(dst[:], src)
             return dst
 
-        def load_scale_rows(queue, plane, scales):
-            for q in range(4):
-                queue.dma_start(plane[32 * q : 32 * q + 4, :].bitcast(I32), scales[0, 4 * q : 4 * q + 4, :].bitcast(I32))
+        def load_scale_rows(plane, scales):
+            for q in range(QUADRANTS):
+                nc.sync.dma_start(plane[32 * q : 32 * q + 4, :].bitcast(I32), scales[0, 4 * q : 4 * q + 4, :].bitcast(I32))
 
-        wt_plane = reused.tile([P, V], U8, name="wt_plane", align_bytes=64, offset=0)
+        def half_of(list_tile, h):
+            return list_tile[:, HALF_COLS * h : HALF_COLS * (h + 1)]
+
+        wt_plane = reused.tile([P, V], U8, name="wt_plane", align_bytes=ALIGN, offset=0)
         xt_plane = tile([P, T], U8, "xt_plane")
         wb_plane = tile([P, N], U8, "wb_plane")
         nc.vector.memset(xt_plane[:].bitcast(I32), 0)
@@ -55,11 +64,11 @@ def tile_list_ownsides_chosen_one_ownpage_kernel(
         list_r = load_list(offs, "list_r")
         list_j = load_list(offs2, "list_j")
         wt_table = tile([P, V], U16, "wt_table")
-        nc.sync.dma_start(wt_table[:].bitcast(I32), wt_words[0].bitcast(I32))
-        load_scale_rows(nc.sync, xt_plane, xt_scales)
+        nc.scalar.dma_start(wt_table[:].bitcast(I32), wt_words[0].bitcast(I32))
+        load_scale_rows(xt_plane, xt_scales)
         xt_table = tile([P, T], U32, "xt_table")
         nc.sync.dma_start(xt_table[:].bitcast(I32), xt_words[0].rearrange("p n t -> p (n t)").bitcast(I32))
-        load_scale_rows(nc.sync, wt_plane, wt_scales)
+        load_scale_rows(wt_plane, wt_scales)
         list_board = load_list(offs3, "list_board")
         list_o = load_list(offs4, "list_o")
         list_u = load_list(offs5, "list_u")
@@ -70,73 +79,76 @@ def tile_list_ownsides_chosen_one_ownpage_kernel(
         nc.sync.dma_start(sb_sb[:], sb.rearrange("(p t) o -> p (t o)", t=PACK))
         wb_codes = tile([P, N], U32, "wb_codes")
         nc.sync.dma_start(wb_codes[:].bitcast(I32), wb_words[0].rearrange("p n t -> p (n t)").bitcast(I32))
-        load_scale_rows(nc.sync, wb_plane, wb_scales)
+        load_scale_rows(wb_plane, wb_scales)
 
         board = [tile([P, C], F32, "board%d" % t) for t in range(PACK)]
         for t in range(PACK):
             nc.vector.memset(board[t][:], 0.0)
 
         w_words = tile([P, R], U16, "w_words")
+        x_words = [tile([P, HALF], U32, "x_words0"), after_wt_plane([P, HALF], U32, "x_words1", 0)]
+        x_bytes = [tile([P, HALF], U8, "x_bytes0"), after_wt_plane([P, HALF], U8, "x_bytes1", 4 * HALF)]
+        dealt_words = [
+            tile([P, PAIR, P], U16, "dealt_words0"),
+            after_wt_plane([P, PAIR, P], U16, "dealt_words1", 5 * HALF),
+        ]
+        dealt_bytes = tile([P, PACK, P], U8, "dealt_bytes")
 
-        def slots(h):
-            return list_j[:, LIST_COLS * h : LIST_COLS * (h + 1)]
+        def deal_words(pair):
+            by_tile = w_words[:].rearrange("p (m t) -> p t m", t=PACK)
+            nc.vector.tensor_copy(dealt_words[pair][:], by_tile[:, PAIR * pair : PAIR * (pair + 1), :])
 
-        def deal(gathered, dealt, lo, hi):
-            nc.vector.tensor_copy(dealt, gathered[:].rearrange("p (m t) -> p t m", t=PACK)[:, lo:hi, :])
-
-        def product(acc, t, h):
+        def first_product(acc, t, h):
             nc.tensor.matmul_mx(
-                acc, lhsT=words[t // 2][:, t % 2, :].bitcast(E2M1), lhsT_scale=scale_bytes[:, t, :],
+                acc, lhsT=dealt_words[t // PAIR][:, t % PAIR, :].bitcast(E2M1), lhsT_scale=dealt_bytes[:, t, :],
                 rhs=x_words[h][:].bitcast(E4M3), rhs_scale=x_bytes[h][:], start=True, stop=True,
             )
 
-        def put(t, h, rows):
-            nc.scalar.activation(board[t][:].indirect(list_board[:, LIST_COLS * h : LIST_COLS * (h + 1)]), rows, COPY)
+        def put(t, h, a_rows):
+            nc.scalar.activation(board[t][:].indirect(half_of(list_board, h)), a_rows, COPY)
 
-        def pick(picked, t, places, weight):
-            nc.scalar.activation(picked[:, t, :], board[t][:].indirect(places[:]), COPY, scale=weight[:, t : t + 1])
+        def pick(dst, t, places, weight):
+            nc.scalar.activation(dst[:, t, :], board[t][:].indirect(places[:]), COPY, scale=weight[:, t : t + 1])
 
-        x_words = [tile([P, HALF], U32, "x_words0"), reused.tile([P, HALF], U32, name="x_words1", align_bytes=64, offset=0)]
-        x_bytes = [tile([P, HALF], U8, "x_bytes0"), reused.tile([P, HALF], U8, name="x_bytes1", align_bytes=64, offset=4 * HALF)]
-        words = [tile([P, 2, P], U16, "dealt_words0"), reused.tile([P, 2, P], U16, name="dealt_words1", align_bytes=64, offset=5 * HALF)]
-        scale_bytes = tile([P, PACK, P], U8, "dealt_bytes")
         nc.vector.tensor_copy(w_words[:], wt_table[:].indirect(list_r[:]))
-        deal(w_words, words[0][:], 0, 2)
-        nc.vector.tensor_copy(x_bytes[0][:], xt_plane[:].indirect(slots(0)))
-        nc.vector.tensor_copy(x_words[0][:], xt_table[:].indirect(slots(0)))
-        nc.vector.tensor_copy(scale_bytes[:].rearrange("p t m -> p m t"), wt_plane[:].indirect(list_r[:]))
-        for t in range(2):
+        nc.vector.tensor_copy(x_bytes[0][:], xt_plane[:].indirect(half_of(list_j, 0)))
+        deal_words(0)
+        nc.vector.tensor_copy(x_words[0][:], xt_table[:].indirect(half_of(list_j, 0)))
+        nc.vector.tensor_copy(dealt_bytes[:].rearrange("p t m -> p m t"), wt_plane[:].indirect(list_r[:]))
+
+        for t in range(PAIR):
             acc = psum.tile([P, HALF], F32, name="a_first%d" % t)
-            product(acc[:], t, 0)
-            rows = tile([P, HALF], F32, "a_rows%d" % t)
+            first_product(acc[:], t, 0)
+            a_rows = tile([P, HALF], F32, "a_rows%d" % t)
             if t == 0:
-                nc.scalar.copy(rows[:], acc[:])
+                nc.scalar.copy(a_rows[:], acc[:])
             else:
-                nc.vector.tensor_copy(rows[:], acc[:])
-            put(t, 0, rows[:])
+                nc.vector.tensor_copy(a_rows[:], acc[:])
+            put(t, 0, a_rows[:])
 
-        deal(w_words, words[1][:], 2, 4)
-        acc = psum.tile([P, 2, HALF], F32, name="a_second")
-        for t in range(2, PACK):
-            product(acc[:, t - 2, :], t, 0)
-        rows = tile([P, 2, HALF], F32, "a_rows_second")
-        nc.vector.tensor_copy(rows[:], acc[:])
-        for t in range(2, PACK):
-            put(t, 0, rows[:, t - 2, :])
+        deal_words(1)
+        acc = psum.tile([P, PAIR, HALF], F32, name="a_second")
+        for t in range(PAIR, PACK):
+            first_product(acc[:, t - PAIR, :], t, 0)
+        a_rows = tile([P, PAIR, HALF], F32, "a_rows_second")
+        nc.vector.tensor_copy(a_rows[:], acc[:])
+        for t in range(PAIR, PACK):
+            put(t, 0, a_rows[:, t - PAIR, :])
 
-        nc.vector.tensor_copy(x_words[1][:], xt_table[:].indirect(slots(1)))
-        nc.vector.tensor_copy(x_bytes[1][:], xt_plane[:].indirect(slots(1)))
+        nc.vector.tensor_copy(x_words[1][:], xt_table[:].indirect(half_of(list_j, 1)))
+        nc.vector.tensor_copy(x_bytes[1][:], xt_plane[:].indirect(half_of(list_j, 1)))
         acc = psum.tile([P, PACK, HALF], F32, name="a_third")
         for t in range(PACK):
-            product(acc[:, t, :], t, 1)
-        rows = tile([P, PACK, HALF], F32, "a_rows_third")
-        nc.vector.tensor_copy(rows[:], acc[:])
+            first_product(acc[:, t, :], t, 1)
+        a_rows = tile([P, PACK, HALF], F32, "a_rows_third")
+        nc.vector.tensor_copy(a_rows[:], acc[:])
         for t in range(PACK):
-            put(t, 1, rows[:, t, :])
+            put(t, 1, a_rows[:, t, :])
+
         picked = [tile([P, PACK, HALF], BF16, "picked0")]
         for t in range(PACK):
             pick(picked[0], t, list_o, sa_sb)
-        picked.append(tile([P, PACK, HALF], BF16, "picked1", tag="sa_sb"))
+        picked.append(tile([P, PACK, HALF], BF16, "picked1", tag="a_rows_third"))
         for t in range(PACK):
             pick(picked[1], t, list_u, sb_sb)
 
@@ -144,10 +156,10 @@ def tile_list_ownsides_chosen_one_ownpage_kernel(
         for b in range(N // P):
             nc.vector.memset(page[b][:], 0.0)
 
-        for h in range(2):
+        for h in range(D // HALF):
             woven = tile([P, HALF, PACK], BF16, "woven%d" % h, tag="woven")
-            for lo in (0, 2):
-                nc.vector.tensor_copy(woven[:, :, lo : lo + 2], picked[h][:, lo : lo + 2, :].rearrange("p t d -> p d t"))
+            for lo in range(0, PACK, PAIR):
+                nc.vector.tensor_copy(woven[:, :, lo : lo + PAIR], picked[h][:, lo : lo + PAIR, :].rearrange("p t d -> p d t"))
             hid_words = tile([P, HALF], U32, "hid_words%d" % h, tag="hid_words")
             hid_bytes = tile([P, HALF], U8, "hid_bytes%d" % h)
             nc.vector.quantize_mx(hid_words[:].bitcast(E4M3), hid_bytes[:], woven[:].rearrange("p d t -> p (d t)"))
@@ -157,16 +169,14 @@ def tile_list_ownsides_chosen_one_ownpage_kernel(
                 both = psum.tile([P, N // P, HALF], F32, name="p_second")
                 accs = [both[:, b, :] for b in range(N // P)]
             for b in range(N // P):
+                cols = slice(P * b, P * (b + 1))
                 nc.tensor.matmul_mx(
-                    accs[b], lhsT=wb_codes[:, P * b : P * (b + 1)].bitcast(E5M2), lhsT_scale=wb_plane[:, P * b : P * (b + 1)],
+                    accs[b], lhsT=wb_codes[:, cols].bitcast(E5M2), lhsT_scale=wb_plane[:, cols],
                     rhs=hid_words[:].bitcast(E4M3), rhs_scale=hid_bytes[:], start=True, stop=True,
                 )
             for b in range(N // P):
-                rows = tile([P, HALF], F32, "p_rows%d_%d" % (h, b))
-                if h == 0 and b == 0:
-                    nc.scalar.copy(rows[:], accs[b])
-                else:
-                    nc.vector.tensor_copy(rows[:], accs[b])
-                nc.scalar.activation(page[b][:].indirect(list_page[:, LIST_COLS * h : LIST_COLS * (h + 1)]), rows[:], COPY)
+                p_rows = tile([P, HALF], F32, "p_rows%d_%d" % (h, b))
+                nc.vector.tensor_copy(p_rows[:], accs[b])
+                nc.scalar.activation(page[b][:].indirect(half_of(list_page, h)), p_rows[:], COPY)
         for b in range(N // P):
             nc.sync.dma_start(out[P * b : P * (b + 1), :], page[b][:])

from contextlib import ExitStack

import concourse.mybir as mybir

F32 = mybir.dt.float32
BF16 = mybir.dt.bfloat16
I32 = mybir.dt.int32
U32 = mybir.dt.uint32
U16 = mybir.dt.uint16
U8 = mybir.dt.uint8
E4M3 = mybir.dt.float8_e4m3fn_x4
E5M2 = mybir.dt.float8_e5m2_x4
E2M1 = mybir.dt.float4_e2m1fn_x4
COPY = mybir.ActivationFunctionType.Copy

K, T, J, R, V, C, D, N, E = 512, 1024, 256, 512, 1024, 512, 256, 256, 512
P = 128
PACK = 4
PAIR = 2
HALF = 128
HALF_COLS = HALF // 16
QUADRANTS = 4
ALIGN = 64

FLOPS = 2 * K * R * J + 2 * R * N * D


def tile_list_ownsides_chosen_one_ownpage_kernel(
    tc, xt_words, xt_scales, wt_words, wt_scales, sa, sb, wb_words, wb_scales,
    offs, offs2, offs3, offs4, offs5, offs6, out,
):
    nc = tc.nc
    with ExitStack() as ctx:
        lists = ctx.enter_context(tc.tile_pool(name="lists", bufs=1))
        pool = ctx.enter_context(tc.tile_pool(name="held", bufs=1))
        reused = ctx.enter_context(tc.tile_pool(name="reused", bufs=1))
        psum = ctx.enter_context(tc.psum_pool(name="psum", bufs=1))

        def tile(shape, dtype, name, tag=None):
            return pool.tile(shape, dtype, name=name, tag=tag or name, bufs=1, align_bytes=ALIGN)

        def after_wt_plane(shape, dtype, name, offset):
            return reused.tile(shape, dtype, name=name, align_bytes=ALIGN, offset=offset)

        def load_list(src, name):
            dst = lists.tile(list(src.shape), U16, name=name)
            nc.sync.dma_start(dst[:], src)
            return dst

        def load_scale_rows(plane, scales):
            for q in range(QUADRANTS):
                nc.sync.dma_start(plane[32 * q : 32 * q + 4, :].bitcast(I32), scales[0, 4 * q : 4 * q + 4, :].bitcast(I32))

        def half_of(list_tile, h):
            return list_tile[:, HALF_COLS * h : HALF_COLS * (h + 1)]

        wt_plane = reused.tile([P, V], U8, name="wt_plane", align_bytes=ALIGN, offset=0)
        xt_plane = tile([P, T], U8, "xt_plane")
        wb_plane = tile([P, N], U8, "wb_plane")
        nc.vector.memset(xt_plane[:].bitcast(I32), 0)
        nc.vector.memset(wt_plane[:].bitcast(I32), 0)
        nc.gpsimd.memset(wb_plane[:].bitcast(I32), 0)

        list_r = load_list(offs, "list_r")
        list_j = load_list(offs2, "list_j")
        wt_table = tile([P, V], U16, "wt_table")
        nc.scalar.dma_start(wt_table[:].bitcast(I32), wt_words[0].bitcast(I32))
        load_scale_rows(xt_plane, xt_scales)
        xt_table = tile([P, T], U32, "xt_table")
        nc.sync.dma_start(xt_table[:].bitcast(I32), xt_words[0].rearrange("p n t -> p (n t)").bitcast(I32))
        load_scale_rows(wt_plane, wt_scales)
        list_board = load_list(offs3, "list_board")
        list_o = load_list(offs4, "list_o")
        list_u = load_list(offs5, "list_u")
        list_page = load_list(offs6, "list_page")
        sa_sb = tile([P, PACK], F32, "sa_sb")
        nc.sync.dma_start(sa_sb[:], sa.rearrange("(p t) o -> p (t o)", t=PACK))
        sb_sb = tile([P, PACK], F32, "sb_sb")
        nc.sync.dma_start(sb_sb[:], sb.rearrange("(p t) o -> p (t o)", t=PACK))
        wb_codes = tile([P, N], U32, "wb_codes")
        nc.sync.dma_start(wb_codes[:].bitcast(I32), wb_words[0].rearrange("p n t -> p (n t)").bitcast(I32))
        load_scale_rows(wb_plane, wb_scales)

        board = [tile([P, C], F32, "board%d" % t) for t in range(PACK)]
        for t in range(PACK):
            nc.vector.memset(board[t][:], 0.0)

        w_words = tile([P, R], U16, "w_words")
        x_words = [tile([P, HALF], U32, "x_words0"), after_wt_plane([P, HALF], U32, "x_words1", 0)]
        x_bytes = [tile([P, HALF], U8, "x_bytes0"), after_wt_plane([P, HALF], U8, "x_bytes1", 4 * HALF)]
        dealt_words = [
            tile([P, PAIR, P], U16, "dealt_words0"),
            after_wt_plane([P, PAIR, P], U16, "dealt_words1", 5 * HALF),
        ]
        dealt_bytes = tile([P, PACK, P], U8, "dealt_bytes")

        def deal_words(pair):
            by_tile = w_words[:].rearrange("p (m t) -> p t m", t=PACK)
            nc.vector.tensor_copy(dealt_words[pair][:], by_tile[:, PAIR * pair : PAIR * (pair + 1), :])

        def first_product(acc, t, h):
            nc.tensor.matmul_mx(
                acc, lhsT=dealt_words[t // PAIR][:, t % PAIR, :].bitcast(E2M1), lhsT_scale=dealt_bytes[:, t, :],
                rhs=x_words[h][:].bitcast(E4M3), rhs_scale=x_bytes[h][:], start=True, stop=True,
            )

        def put(t, h, a_rows):
            nc.scalar.activation(board[t][:].indirect(half_of(list_board, h)), a_rows, COPY)

        def pick(dst, t, places, weight):
            nc.scalar.activation(dst[:, t, :], board[t][:].indirect(places[:]), COPY, scale=weight[:, t : t + 1])

        nc.vector.tensor_copy(w_words[:], wt_table[:].indirect(list_r[:]))
        nc.vector.tensor_copy(x_bytes[0][:], xt_plane[:].indirect(half_of(list_j, 0)))
        deal_words(0)
        nc.vector.tensor_copy(x_words[0][:], xt_table[:].indirect(half_of(list_j, 0)))
        nc.vector.tensor_copy(dealt_bytes[:].rearrange("p t m -> p m t"), wt_plane[:].indirect(list_r[:]))

        for t in range(PAIR):
            acc = psum.tile([P, HALF], F32, name="a_first%d" % t)
            first_product(acc[:], t, 0)
            a_rows = tile([P, HALF], F32, "a_rows%d" % t)
            if t == 0:
                nc.scalar.copy(a_rows[:], acc[:])
            else:
                nc.vector.tensor_copy(a_rows[:], acc[:])
            put(t, 0, a_rows[:])

        deal_words(1)
        acc = psum.tile([P, PAIR, HALF], F32, name="a_second")
        for t in range(PAIR, PACK):
            first_product(acc[:, t - PAIR, :], t, 0)
        a_rows = tile([P, PAIR, HALF], F32, "a_rows_second")
        nc.vector.tensor_copy(a_rows[:], acc[:])
        for t in range(PAIR, PACK):
            put(t, 0, a_rows[:, t - PAIR, :])

        nc.vector.tensor_copy(x_words[1][:], xt_table[:].indirect(half_of(list_j, 1)))
        nc.vector.tensor_copy(x_bytes[1][:], xt_plane[:].indirect(half_of(list_j, 1)))
        acc = psum.tile([P, PACK, HALF], F32, name="a_third")
        for t in range(PACK):
            first_product(acc[:, t, :], t, 1)
        a_rows = tile([P, PACK, HALF], F32, "a_rows_third")
        nc.vector.tensor_copy(a_rows[:], acc[:])
        for t in range(PACK):
            put(t, 1, a_rows[:, t, :])

        picked = [tile([P, PACK, HALF], BF16, "picked0")]
        for t in range(PACK):
            pick(picked[0], t, list_o, sa_sb)
        picked.append(tile([P, PACK, HALF], BF16, "picked1", tag="a_rows_third"))
        for t in range(PACK):
            pick(picked[1], t, list_u, sb_sb)

        page = [tile([P, E], F32, "page%d" % b, tag=("dealt_words0", "dealt_bytes")[b]) for b in range(N // P)]
        for b in range(N // P):
            nc.vector.memset(page[b][:], 0.0)

        for h in range(D // HALF):
            woven = tile([P, HALF, PACK], BF16, "woven%d" % h, tag="woven")
            for lo in range(0, PACK, PAIR):
                nc.vector.tensor_copy(woven[:, :, lo : lo + PAIR], picked[h][:, lo : lo + PAIR, :].rearrange("p t d -> p d t"))
            hid_words = tile([P, HALF], U32, "hid_words%d" % h, tag="hid_words")
            hid_bytes = tile([P, HALF], U8, "hid_bytes%d" % h)
            nc.vector.quantize_mx(hid_words[:].bitcast(E4M3), hid_bytes[:], woven[:].rearrange("p d t -> p (d t)"))
            if h == 0:
                accs = [psum.tile([P, HALF], F32, name="p_first%d" % b)[:] for b in range(N // P)]
            else:
                both = psum.tile([P, N // P, HALF], F32, name="p_second")
                accs = [both[:, b, :] for b in range(N // P)]
            for b in range(N // P):
                cols = slice(P * b, P * (b + 1))
                nc.tensor.matmul_mx(
                    accs[b], lhsT=wb_codes[:, cols].bitcast(E5M2), lhsT_scale=wb_plane[:, cols],
                    rhs=hid_words[:].bitcast(E4M3), rhs_scale=hid_bytes[:], start=True, stop=True,
                )
            for b in range(N // P):
                p_rows = tile([P, HALF], F32, "p_rows%d_%d" % (h, b))
                nc.vector.tensor_copy(p_rows[:], accs[b])
                nc.scalar.activation(page[b][:].indirect(half_of(list_page, h)), p_rows[:], COPY)
        for b in range(N // P):
            nc.sync.dma_start(out[P * b : P * (b + 1), :], page[b][:])
